import numpy as np
import ml_dtypes


def mxq(x, axis, fmt="e4m3"):
    dtype, down = {"e4m3": (ml_dtypes.float8_e4m3fn, 7), "e5m2": (ml_dtypes.float8_e5m2, 14)}[fmt]
    v = np.moveaxis(np.asarray(x, np.float32).astype(ml_dtypes.bfloat16).astype(np.float64), axis, -1)
    blocks = v.reshape(v.shape[:-1] + (-1, 32))
    amax = np.abs(blocks).max(-1, keepdims=True)
    byte = np.maximum(np.where(amax > 0, np.frexp(amax)[1] - 1 + 127, 0) - down, 1)
    scale = np.exp2(byte - 127.0)
    codes = (blocks / scale).astype(np.float32).astype(dtype).astype(np.float64)
    return np.moveaxis((codes * scale).reshape(v.shape), -1, axis)


WIDE = False


def mx_kscale(k):
    if not WIDE:
        return np.ones(k)
    levels = np.array([10, -10, 5, -5, 0])
    if k % 512:
        return np.exp2(np.random.permutation(np.resize(levels, k // 32))).repeat(32)
    a = np.empty((k // 512, 16))
    for p in range(k // 512):
        a[p, :8] = np.random.permutation(np.resize(levels, 8))
        for g in range(8):
            far = levels[np.abs(levels - a[p, g]) >= 10]
            a[p, g + 8] = far[np.random.randint(len(far))]
    return np.exp2(a.ravel()).repeat(32)


def f64(x):
    return np.asarray(x).astype(np.float64)


def striped(idx):
    return np.tile(idx.reshape(-1, 16).T, (8, 1)).astype(np.uint16)


def unstriped(offs):
    return offs[:16].T.reshape(-1).astype(np.int64)


def silu(v):
    return v / (1.0 + np.exp(-np.maximum(v, -700.0)))


K, T, E, C, N = 1024, 2048, 4, 128, 256


def by_expert(wq, xq):
    return np.concatenate([wq[e].T @ xq[:, e * C:(e + 1) * C] for e in range(E)], axis=1)


def setup_inputs():
    n = np.random.standard_normal
    s = mx_kscale(K)[:, None]
    return {
        "xT": (n((K, T)) * s).astype(np.float32),
        "w": (n((E, K, N)) / np.sqrt(K) / s[None]).astype(np.float32),
        "b": (0.3 * n((N, E))).astype(np.float32),
        "gate": np.tile(np.random.uniform(0.2, 1.0, E * C), (N, 1)).astype(np.float32),
        "offs": striped(np.random.permutation(T)[:E * C]),
    }


def reference(xT, w, b, gate, offs):
    idx = unstriped(offs)
    xq = mxq(f64(xT)[:, idx], 0, "e4m3")
    y = by_expert(mxq(f64(w), 1, "e4m3"), xq)
    y = silu(y + np.repeat(f64(b), C, axis=1))
    out = np.zeros((N, T))
    out[:, idx] = f64(gate) * y
    return out

@@ -1,0 +1,143 @@
+from contextlib import ExitStack
+
+import concourse.mybir as mybir
+
+K, T, E, C, N = 1024, 2048, 4, 128, 256
+FLOPS = 2 * K * N * E * C
+
+F32 = mybir.dt.float32
+BF16 = mybir.dt.bfloat16
+U32 = mybir.dt.uint32
+U16 = mybir.dt.uint16
+U8 = mybir.dt.uint8
+FP8X4 = mybir.dt.float8_e4m3fn_x4
+SILU = mybir.ActivationFunctionType.Silu
+MULT = mybir.AluOpType.mult
+
+P = 128
+PACK = 4
+K_PASS = P * PACK
+PASSES = K // K_PASS
+BLOCKS = N // P
+SLOTS = E * C
+RUN = 4
+HALF = 256
+HALVES = E * C // HALF
+COLS = HALF // 16
+
+SCATTERS_AFTER = {0: (), 1: ((0, 0),), 2: (), 3: ((0, 1), (1, 0), (1, 1))}
+DIRECT = (False, True)
+
+
+def tile_routed_moe_kernel(tc, xT, w, b, gate, offs, out):
+    nc = tc.nc
+    with ExitStack() as ctx:
+        held = ctx.enter_context(tc.tile_pool(name="held", bufs=1))
+        psum = ctx.enter_context(tc.psum_pool(name="psum", bufs=1))
+
+        offs_sb = held.tile([P, E * C // 16], U16, name="offs_sb")
+        nc.sync.dma_start(offs_sb[:], offs)
+
+        bias = held.tile([P, BLOCKS, E], F32, name="bias")
+        nc.scalar.dma_start(out=bias[:], in_=b.rearrange("(nb p) e -> p nb e", p=P))
+
+        planes = {}
+        x_view = xT.rearrange("(g p t) n -> g p t n", p=P, t=PACK)
+        for g in range(PASSES):
+            for t in range(PACK):
+                planes[g, t] = held.tile([P, T], F32, name="plane%d%d" % (g, t))
+                nc.sync.dma_start(out=planes[g, t][:], in_=x_view[g, :, t, :])
+
+        w_raw = {}
+        gate_sb = {}
+        for e in range(E):
+            for g in range(PASSES):
+                w_raw[e, g] = held.tile([P, PACK, N], F32, name="wraw%d%d" % (e, g))
+                nc.sync.dma_start(
+                    out=w_raw[e, g][:],
+                    in_=w[e, g * K_PASS : (g + 1) * K_PASS, :].rearrange("(p j) n -> p j n", j=PACK),
+                )
+            if e % 2 == 1:
+                nb = e // 2
+                gate_sb[nb] = held.tile([P, SLOTS], F32, name="gate%d" % nb)
+                nc.sync.dma_start(out=gate_sb[nb][:], in_=gate[nb * P : (nb + 1) * P, :])
+
+        warm = held.tile([P, 1], F32, name="warm")
+        warm2 = held.tile([P, 1], F32, name="warm2")
+        nc.vector.memset(warm[:], 0.0)
+        nc.scalar.activation(out=warm2[:], in_=warm[:], func=SILU)
+        window = {}
+        for nb in range(BLOCKS):
+            window[nb] = held.tile([P, T], F32, name="window%d" % nb)
+            nc.vector.memset(window[nb][:], 0.0)
+
+        x_codes = {}
+        x_scales = {}
+        for g in range(PASSES):
+            x_grouped = held.tile([P, SLOTS, PACK], BF16, name="xg%d" % g, align_bytes=64)
+            if not DIRECT[g]:
+                picked = held.tile([P, PACK, SLOTS], F32, name="picked%d" % g)
+            for t in range(PACK):
+                nc.vector.tensor_copy(
+                    out=x_grouped[:, :, t] if DIRECT[g] else picked[:, t, :],
+                    in_=planes[g, t][:].indirect(offs_sb[:]),
+                )
+            if not DIRECT[g]:
+                nc.scalar.copy(
+                    out=x_grouped[:].rearrange("p (c i) t -> p c t i", i=RUN),
+                    in_=picked[:].rearrange("p t (c i) -> p c t i", i=RUN),
+                )
+            x_codes[g] = held.tile([P, SLOTS], U32, name="xc%d" % g, align_bytes=64)
+            x_scales[g] = held.tile([P, SLOTS], U8, name="xs%d" % g, align_bytes=64)
+            nc.vector.quantize_mx(
+                out=x_codes[g][:].bitcast(FP8X4),
+                scales=x_scales[g][:],
+                in_=x_grouped[:].rearrange("p c t -> p (c t)"),
+            )
+
+        y = {}
+        for e in range(E):
+            h = e // 2
+            lo = (e % 2) * C
+            w_codes = {}
+            w_scales = {}
+            for g in range(PASSES):
+                w_grouped = held.tile([P, N, PACK], BF16, name="wg%d%d" % (e, g), align_bytes=64)
+                copier = nc.vector if g == PASSES - 1 and e % 2 == 1 else nc.any
+                copier.tensor_copy(
+                    out=w_grouped[:].rearrange("p (c i) j -> p c j i", i=RUN),
+                    in_=w_raw[e, g][:].rearrange("p j (c i) -> p c j i", i=RUN),
+                )
+                w_codes[g] = held.tile([P, N], U32, name="wc%d%d" % (e, g), align_bytes=64)
+                w_scales[g] = held.tile([P, N], U8, name="ws%d%d" % (e, g), align_bytes=64)
+                nc.vector.quantize_mx(
+                    out=w_codes[g][:].bitcast(FP8X4),
+                    scales=w_scales[g][:],
+                    in_=w_grouped[:].rearrange("p n j -> p (n j)"),
+                )
+            for nb in range(BLOCKS):
+                if e % 2 == 0:
+                    y[nb, h] = held.tile([P, HALF], F32, name="y%d%d" % (nb, h))
+                acc = psum.tile([P, C], F32, name="acc%d%d" % (e, nb))
+                for g in range(PASSES):
+                    nc.tensor.matmul_mx(
+                        out=acc[:],
+                        lhsT=w_codes[g][:, nb * P : (nb + 1) * P].bitcast(FP8X4),
+                        lhsT_scale=w_scales[g][:, nb * P : (nb + 1) * P],
+                        rhs=x_codes[g][:, e * C : (e + 1) * C].bitcast(FP8X4),
+                        rhs_scale=x_scales[g][:, e * C : (e + 1) * C],
+                        start=(g == 0),
+                        stop=(g == PASSES - 1),
+                    )
+                nc.scalar.activation(
+                    out=y[nb, h][:, lo : lo + C], in_=acc[:], func=SILU, bias=bias[:, nb, e : e + 1], scale=1.0
+                )
+            for nb, hh in SCATTERS_AFTER[e]:
+                nc.vector.tensor_tensor(
+                    out=window[nb][:].indirect(offs_sb[:, hh * COLS : (hh + 1) * COLS]),
+                    in0=y[nb, hh][:],
+                    in1=gate_sb[nb][:, hh * HALF : (hh + 1) * HALF],
+                    op=MULT,
+                )
+                if hh == HALVES - 1:
+                    nc.sync.dma_start(out=out[nb * P : (nb + 1) * P, :], in_=window[nb][:])

@@ -20,7 +20,7 @@ K_PASS = P * PACK
 PASSES = K // K_PASS
 BLOCKS = N // P
 SLOTS = E * C
-RUN = 4
+RUN = 8
 HALF = 256
 HALVES = E * C // HALF
 COLS = HALF // 16

@@ -26,6 +26,7 @@ HALVES = E * C // HALF
 COLS = HALF // 16
 
 SCATTERS_AFTER = {0: (), 1: ((0, 0),), 2: (), 3: ((0, 1), (1, 0), (1, 1))}
+DMA_ALIGN = 256
 DIRECT = (False, True)
 
 
@@ -45,21 +46,21 @@ def tile_routed_moe_kernel(tc, xT, w, b, gate, offs, out):
         x_view = xT.rearrange("(g p t) n -> g p t n", p=P, t=PACK)
         for g in range(PASSES):
             for t in range(PACK):
-                planes[g, t] = held.tile([P, T], F32, name="plane%d%d" % (g, t))
+                planes[g, t] = held.tile([P, T], F32, name="plane%d%d" % (g, t), align_bytes=DMA_ALIGN)
                 nc.sync.dma_start(out=planes[g, t][:], in_=x_view[g, :, t, :])
 
         w_raw = {}
         gate_sb = {}
         for e in range(E):
             for g in range(PASSES):
-                w_raw[e, g] = held.tile([P, PACK, N], F32, name="wraw%d%d" % (e, g))
+                w_raw[e, g] = held.tile([P, PACK, N], F32, name="wraw%d%d" % (e, g), align_bytes=DMA_ALIGN)
                 nc.sync.dma_start(
                     out=w_raw[e, g][:],
                     in_=w[e, g * K_PASS : (g + 1) * K_PASS, :].rearrange("(p j) n -> p j n", j=PACK),
                 )
             if e % 2 == 1:
                 nb = e // 2
-                gate_sb[nb] = held.tile([P, SLOTS], F32, name="gate%d" % nb)
+                gate_sb[nb] = held.tile([P, SLOTS], F32, name="gate%d" % nb, align_bytes=DMA_ALIGN)
                 nc.sync.dma_start(out=gate_sb[nb][:], in_=gate[nb * P : (nb + 1) * P, :])
 
         warm = held.tile([P, 1], F32, name="warm")
@@ -68,7 +69,7 @@ def tile_routed_moe_kernel(tc, xT, w, b, gate, offs, out):
         nc.scalar.activation(out=warm2[:], in_=warm[:], func=SILU)
         window = {}
         for nb in range(BLOCKS):
-            window[nb] = held.tile([P, T], F32, name="window%d" % nb)
+            window[nb] = held.tile([P, T], F32, name="window%d" % nb, align_bytes=DMA_ALIGN)
             nc.vector.memset(window[nb][:], 0.0)
 
         x_codes = {}

@@ -39,7 +39,7 @@ def tile_routed_moe_kernel(tc, xT, w, b, gate, offs, out):
         offs_sb = held.tile([P, E * C // 16], U16, name="offs_sb")
         nc.sync.dma_start(offs_sb[:], offs)
 
-        bias = held.tile([P, BLOCKS, E], F32, name="bias")
+        bias = held.tile([P, BLOCKS, E], F32, name="bias", align_bytes=DMA_ALIGN)
         nc.scalar.dma_start(out=bias[:], in_=b.rearrange("(nb p) e -> p nb e", p=P))
 
         planes = {}
@@ -75,9 +75,9 @@ def tile_routed_moe_kernel(tc, xT, w, b, gate, offs, out):
         x_codes = {}
         x_scales = {}
         for g in range(PASSES):
-            x_grouped = held.tile([P, SLOTS, PACK], BF16, name="xg%d" % g, align_bytes=64)
+            x_grouped = held.tile([P, SLOTS, PACK], BF16, name="xg%d" % g, align_bytes=DMA_ALIGN)
             if not DIRECT[g]:
-                picked = held.tile([P, PACK, SLOTS], F32, name="picked%d" % g)
+                picked = held.tile([P, PACK, SLOTS], F32, name="picked%d" % g, align_bytes=DMA_ALIGN)
             for t in range(PACK):
                 nc.vector.tensor_copy(
                     out=x_grouped[:, :, t] if DIRECT[g] else picked[:, t, :],
@@ -88,8 +88,8 @@ def tile_routed_moe_kernel(tc, xT, w, b, gate, offs, out):
                     out=x_grouped[:].rearrange("p (c i) t -> p c t i", i=RUN),
                     in_=picked[:].rearrange("p t (c i) -> p c t i", i=RUN),
                 )
-            x_codes[g] = held.tile([P, SLOTS], U32, name="xc%d" % g, align_bytes=64)
-            x_scales[g] = held.tile([P, SLOTS], U8, name="xs%d" % g, align_bytes=64)
+            x_codes[g] = held.tile([P, SLOTS], U32, name="xc%d" % g, align_bytes=DMA_ALIGN)
+            x_scales[g] = held.tile([P, SLOTS], U8, name="xs%d" % g, align_bytes=DMA_ALIGN)
             nc.vector.quantize_mx(
                 out=x_codes[g][:].bitcast(FP8X4),
                 scales=x_scales[g][:],
@@ -103,14 +103,14 @@ def tile_routed_moe_kernel(tc, xT, w, b, gate, offs, out):
             w_codes = {}
             w_scales = {}
             for g in range(PASSES):
-                w_grouped = held.tile([P, N, PACK], BF16, name="wg%d%d" % (e, g), align_bytes=64)
+                w_grouped = held.tile([P, N, PACK], BF16, name="wg%d%d" % (e, g), align_bytes=DMA_ALIGN)
                 copier = nc.vector if g == PASSES - 1 and e % 2 == 1 else nc.any
                 copier.tensor_copy(
                     out=w_grouped[:].rearrange("p (c i) j -> p c j i", i=RUN),
                     in_=w_raw[e, g][:].rearrange("p j (c i) -> p c j i", i=RUN),
                 )
-                w_codes[g] = held.tile([P, N], U32, name="wc%d%d" % (e, g), align_bytes=64)
-                w_scales[g] = held.tile([P, N], U8, name="ws%d%d" % (e, g), align_bytes=64)
+                w_codes[g] = held.tile([P, N], U32, name="wc%d%d" % (e, g), align_bytes=DMA_ALIGN)
+                w_scales[g] = held.tile([P, N], U8, name="ws%d%d" % (e, g), align_bytes=DMA_ALIGN)
                 nc.vector.quantize_mx(
                     out=w_codes[g][:].bitcast(FP8X4),
                     scales=w_scales[g][:],
@@ -118,7 +118,7 @@ def tile_routed_moe_kernel(tc, xT, w, b, gate, offs, out):
                 )
             for nb in range(BLOCKS):
                 if e % 2 == 0:
-                    y[nb, h] = held.tile([P, HALF], F32, name="y%d%d" % (nb, h))
+                    y[nb, h] = held.tile([P, HALF], F32, name="y%d%d" % (nb, h), align_bytes=DMA_ALIGN)
                 acc = psum.tile([P, C], F32, name="acc%d%d" % (e, nb))
                 for g in range(PASSES):
                     nc.tensor.matmul_mx(

@@ -22,12 +22,71 @@ BLOCKS = N // P
 SLOTS = E * C
 RUN = 8
 HALF = 256
-HALVES = E * C // HALF
+HALVES = SLOTS // HALF
 COLS = HALF // 16
-
-SCATTERS_AFTER = {0: (), 1: ((0, 0),), 2: (), 3: ((0, 1), (1, 0), (1, 1))}
 DMA_ALIGN = 256
 DIRECT = (False, True)
+LOADS = (
+    ("x", 0, 0),
+    ("x", 0, 1),
+    ("x", 0, 2),
+    ("x", 0, 3),
+    ("x", 1, 0),
+    ("x", 1, 1),
+    ("x", 1, 2),
+    ("x", 1, 3),
+    (0, None),
+    (1, None),
+    ("gate", 0, 0, 2),
+    (2, None),
+    (3, 0),
+    (3, 1),
+    ("gate", 1, 0, 2),
+)
+TOKENS = (
+    ("gather", 0, 0, 0, 2),
+    ("gather", 0, 1, 0, 2),
+    ("gather", 0, 2, 0, 2),
+    ("gather", 0, 3, 0, 2),
+    ("interleave", 0),
+    ("xq", 0, 0, 2),
+    ("gather", 1, 0, 0, 2),
+    ("gather", 1, 1, 0, 2),
+    ("gather", 1, 2, 0, 2),
+    ("gather", 1, 3, 0, 2),
+    ("xq", 1, 0, 2),
+)
+WORK = (
+    ("cw", 0, 0, "s"),
+    ("qw", 0, 0),
+    ("cw", 0, 1, "s"),
+    ("qw", 0, 1),
+    ("mm", 0, 0),
+    ("mm", 0, 1),
+    ("cw", 1, 0, "s"),
+    ("qw", 1, 0),
+    ("cw", 1, 1, "v"),
+    ("qw", 1, 1),
+    ("mm", 1, 0),
+    ("mm", 1, 1),
+    ("scatter", 0, 0),
+    ("cw", 2, 0, "v"),
+    ("qw", 2, 0),
+    ("cw", 2, 1, "s"),
+    ("qw", 2, 1),
+    ("mm", 2, 0),
+    ("mm", 2, 1),
+    ("cb", 3, 0, 0, 2, "s"),
+    ("qb", 3, 0, 0, 2),
+    ("mm", 3, 0),
+    ("scatter", 0, 1),
+    ("cb", 3, 1, 0, 2, "s"),
+    ("qb", 3, 1, 0, 2),
+    ("mm", 3, 1),
+    ("scatter", 1, 0),
+    ("scatter", 1, 1),
+)
+TURN = (1, 0)
 
 
 def tile_routed_moe_kernel(tc, xT, w, b, gate, offs, out):
@@ -36,7 +95,7 @@ def tile_routed_moe_kernel(tc, xT, w, b, gate, offs, out):
         held = ctx.enter_context(tc.tile_pool(name="held", bufs=1))
         psum = ctx.enter_context(tc.psum_pool(name="psum", bufs=1))
 
-        offs_sb = held.tile([P, E * C // 16], U16, name="offs_sb")
+        offs_sb = held.tile([P, SLOTS // 16], U16, name="offs_sb")
         nc.sync.dma_start(offs_sb[:], offs)
 
         bias = held.tile([P, BLOCKS, E], F32, name="bias", align_bytes=DMA_ALIGN)
@@ -44,24 +103,36 @@ def tile_routed_moe_kernel(tc, xT, w, b, gate, offs, out):
 
         planes = {}
         x_view = xT.rearrange("(g p t) n -> g p t n", p=P, t=PACK)
-        for g in range(PASSES):
-            for t in range(PACK):
-                planes[g, t] = held.tile([P, T], F32, name="plane%d%d" % (g, t), align_bytes=DMA_ALIGN)
-                nc.sync.dma_start(out=planes[g, t][:], in_=x_view[g, :, t, :])
-
         w_raw = {}
         gate_sb = {}
-        for e in range(E):
-            for g in range(PASSES):
-                w_raw[e, g] = held.tile([P, PACK, N], F32, name="wraw%d%d" % (e, g), align_bytes=DMA_ALIGN)
+        w_view = w.rearrange("e (g p j) n -> e g p j n", p=P, j=PACK)
+        for item in LOADS:
+            if item[0] == "x":
+                g, t = item[1:]
+                planes[g, t] = held.tile([P, T], F32, name="plane%d%d" % (g, t), align_bytes=DMA_ALIGN)
+                nc.sync.dma_start(out=planes[g, t][:], in_=x_view[g, :, t, :])
+            elif item[0] == "gate":
+                nb = item[1]
+                lo, hi = item[2:]
+                if nb not in gate_sb:
+                    gate_sb[nb] = held.tile([P, SLOTS], F32, name="gate%d" % nb, align_bytes=DMA_ALIGN)
                 nc.sync.dma_start(
-                    out=w_raw[e, g][:],
-                    in_=w[e, g * K_PASS : (g + 1) * K_PASS, :].rearrange("(p j) n -> p j n", j=PACK),
+                    out=gate_sb[nb][:, lo * HALF : hi * HALF],
+                    in_=gate[nb * P : (nb + 1) * P, lo * HALF : hi * HALF],
                 )
-            if e % 2 == 1:
-                nb = e // 2
-                gate_sb[nb] = held.tile([P, SLOTS], F32, name="gate%d" % nb, align_bytes=DMA_ALIGN)
-                nc.sync.dma_start(out=gate_sb[nb][:], in_=gate[nb * P : (nb + 1) * P, :])
+            elif item[1] is None:
+                e = item[0]
+                for g in range(PASSES):
+                    w_raw[e, g, None] = held.tile([P, PACK, N], F32, name="wraw%d_%d" % (e, g), align_bytes=DMA_ALIGN)
+                    nc.sync.dma_start(out=w_raw[e, g, None][:], in_=w_view[e, g])
+            else:
+                e, nb = item
+                for g in range(PASSES):
+                    if (e, nb) not in w_raw:
+                        w_raw[e, nb] = held.tile([P, PASSES, PACK, P], F32, name="wraw%d%d" % (e, nb), align_bytes=DMA_ALIGN)
+                    nc.sync.dma_start(
+                        out=w_raw[e, nb][:, g, :, :], in_=w_view[e, g, :, :, nb * P : (nb + 1) * P]
+                    )
 
         warm = held.tile([P, 1], F32, name="warm")
         warm2 = held.tile([P, 1], F32, name="warm2")
@@ -72,73 +143,146 @@ def tile_routed_moe_kernel(tc, xT, w, b, gate, offs, out):
             window[nb] = held.tile([P, T], F32, name="window%d" % nb, align_bytes=DMA_ALIGN)
             nc.vector.memset(window[nb][:], 0.0)
 
+        engines = {"v": nc.vector, "s": nc.scalar, "a": nc.any, "p": nc.gpsimd}
+
+        def copy(engine, out_view, in_view):
+            if engine == "s":
+                nc.scalar.copy(out=out_view, in_=in_view)
+            elif engine == "p":
+                nc.gpsimd.tensor_scalar(
+                    out=out_view, in0=in_view, scalar1=1.0, scalar2=0.0, op0=MULT, op1=mybir.AluOpType.add
+                )
+            else:
+                engines[engine].tensor_copy(out=out_view, in_=in_view)
+
+        x_grouped = {}
         x_codes = {}
         x_scales = {}
+        picked = held.tile([P, PACK, SLOTS], F32, name="picked0", align_bytes=DMA_ALIGN)
         for g in range(PASSES):
-            x_grouped = held.tile([P, SLOTS, PACK], BF16, name="xg%d" % g, align_bytes=DMA_ALIGN)
-            if not DIRECT[g]:
-                picked = held.tile([P, PACK, SLOTS], F32, name="picked%d" % g, align_bytes=DMA_ALIGN)
-            for t in range(PACK):
-                nc.vector.tensor_copy(
-                    out=x_grouped[:, :, t] if DIRECT[g] else picked[:, t, :],
-                    in_=planes[g, t][:].indirect(offs_sb[:]),
-                )
-            if not DIRECT[g]:
-                nc.scalar.copy(
-                    out=x_grouped[:].rearrange("p (c i) t -> p c t i", i=RUN),
-                    in_=picked[:].rearrange("p t (c i) -> p c t i", i=RUN),
-                )
-            x_codes[g] = held.tile([P, SLOTS], U32, name="xc%d" % g, align_bytes=DMA_ALIGN)
-            x_scales[g] = held.tile([P, SLOTS], U8, name="xs%d" % g, align_bytes=DMA_ALIGN)
-            nc.vector.quantize_mx(
-                out=x_codes[g][:].bitcast(FP8X4),
-                scales=x_scales[g][:],
-                in_=x_grouped[:].rearrange("p c t -> p (c t)"),
+            x_grouped[g] = held.tile([P, SLOTS, PACK], BF16, name="xg%d" % g, align_bytes=DMA_ALIGN)
+        y = {}
+        for h in range(HALVES):
+            for nb in range(BLOCKS):
+                y[h, nb] = held.tile([P, HALF], F32, name="y%d%d" % (nb, h), align_bytes=DMA_ALIGN)
+        grouped = {}
+        codes = {}
+        scales = {}
+
+        def gather(g, t, lo, hi):
+            s = slice(lo * HALF, hi * HALF)
+            nc.vector.tensor_copy(
+                out=x_grouped[g][:, s, t] if g == 1 else picked[:, t, s],
+                in_=planes[g, t][:].indirect(offs_sb[:, lo * COLS : hi * COLS]),
             )
 
-        y = {}
-        for e in range(E):
-            h = e // 2
-            lo = (e % 2) * C
-            w_codes = {}
-            w_scales = {}
+        def interleave(g):
+            nc.scalar.copy(
+                out=x_grouped[g][:].rearrange("p (c i) t -> p c t i", i=RUN),
+                in_=picked[:].rearrange("p t (c i) -> p c t i", i=RUN),
+            )
+
+        def quantise_tokens(g, lo, hi, pinned=False):
+            s = slice(lo * HALF, hi * HALF)
+            width = (hi - lo) * HALF
+            if pinned:
+                xc = held.tile([P, width], U32, name="xc%d%d" % (g, lo), tag="turn", align_bytes=DMA_ALIGN)
+            else:
+                xc = held.tile([P, width], U32, name="xc%d%d" % (g, lo), align_bytes=DMA_ALIGN)
+            xs = held.tile([P, width], U8, name="xs%d%d" % (g, lo), align_bytes=DMA_ALIGN)
+            nc.vector.quantize_mx(
+                out=xc[:].bitcast(FP8X4),
+                scales=xs[:],
+                in_=x_grouped[g][:, s, :].rearrange("p c t -> p (c t)"),
+            )
+            for h in range(lo, hi):
+                x_codes[g, h] = xc[:, (h - lo) * HALF : (h - lo + 1) * HALF]
+                x_scales[g, h] = xs[:, (h - lo) * HALF : (h - lo + 1) * HALF]
+
+        def copy_whole(e, g, engine):
+            grouped[e, g, None] = held.tile([P, N, PACK], BF16, name="wg%d_%d" % (e, g), align_bytes=DMA_ALIGN)
+            copy(
+                engine,
+                grouped[e, g, None][:].rearrange("p (c i) j -> p c j i", i=RUN),
+                w_raw[e, g, None][:].rearrange("p j (c i) -> p c j i", i=RUN),
+            )
+
+        def quantise_whole(e, g):
+            codes[e, g, None] = held.tile([P, N], U32, name="wc%d_%d" % (e, g), align_bytes=DMA_ALIGN)
+            scales[e, g, None] = held.tile([P, N], U8, name="ws%d_%d" % (e, g), align_bytes=DMA_ALIGN)
+            nc.vector.quantize_mx(
+                out=codes[e, g, None][:].bitcast(FP8X4),
+                scales=scales[e, g, None][:],
+                in_=grouped[e, g, None][:].rearrange("p n j -> p (n j)"),
+            )
+
+        def copy_block(e, nb, lo, hi, engine):
+            if (e, nb) not in grouped:
+                if (e, nb) == TURN:
+                    grouped[e, nb] = held.tile([P, PASSES, P, PACK], BF16, name="wg%d%d" % (e, nb), tag="turn", align_bytes=DMA_ALIGN)
+                else:
+                    grouped[e, nb] = held.tile([P, PASSES, P, PACK], BF16, name="wg%d%d" % (e, nb), align_bytes=DMA_ALIGN)
+            copy(
+                engine,
+                grouped[e, nb][:, lo:hi].rearrange("p g (c i) j -> p g c j i", i=RUN),
+                w_raw[e, nb][:, lo:hi].rearrange("p g j (c i) -> p g c j i", i=RUN),
+            )
+
+        def quantise_block(e, nb, lo, hi):
+            if (e, nb) not in codes:
+                codes[e, nb] = held.tile([P, PASSES * P], U32, name="wc%d%d" % (e, nb), align_bytes=DMA_ALIGN)
+                scales[e, nb] = held.tile([P, PASSES * P], U8, name="ws%d%d" % (e, nb), align_bytes=DMA_ALIGN)
+            s = slice(lo * P, hi * P)
+            nc.vector.quantize_mx(
+                out=codes[e, nb][:, s].bitcast(FP8X4),
+                scales=scales[e, nb][:, s],
+                in_=grouped[e, nb][:, lo:hi].rearrange("p g n j -> p (g n j)"),
+            )
+
+        def multiply(e, nb):
+            acc = psum.tile([P, C], F32, name="acc%d%d" % (e, nb))
             for g in range(PASSES):
-                w_grouped = held.tile([P, N, PACK], BF16, name="wg%d%d" % (e, g), align_bytes=DMA_ALIGN)
-                copier = nc.vector if g == PASSES - 1 and e % 2 == 1 else nc.any
-                copier.tensor_copy(
-                    out=w_grouped[:].rearrange("p (c i) j -> p c j i", i=RUN),
-                    in_=w_raw[e, g][:].rearrange("p j (c i) -> p c j i", i=RUN),
+                if (e, nb) in codes:
+                    key, s = (e, nb), slice(g * P, (g + 1) * P)
+                else:
+                    key, s = (e, g, None), slice(nb * P, (nb + 1) * P)
+                nc.tensor.matmul_mx(
+                    out=acc[:],
+                    lhsT=codes[key][:, s].bitcast(FP8X4),
+                    lhsT_scale=scales[key][:, s],
+                    rhs=x_codes[g, e // 2][:, (e % 2) * C : (e % 2 + 1) * C].bitcast(FP8X4),
+                    rhs_scale=x_scales[g, e // 2][:, (e % 2) * C : (e % 2 + 1) * C],
+                    start=(g == 0),
+                    stop=(g == PASSES - 1),
                 )
-                w_codes[g] = held.tile([P, N], U32, name="wc%d%d" % (e, g), align_bytes=DMA_ALIGN)
-                w_scales[g] = held.tile([P, N], U8, name="ws%d%d" % (e, g), align_bytes=DMA_ALIGN)
-                nc.vector.quantize_mx(
-                    out=w_codes[g][:].bitcast(FP8X4),
-                    scales=w_scales[g][:],
-                    in_=w_grouped[:].rearrange("p n j -> p (n j)"),
-                )
-            for nb in range(BLOCKS):
-                if e % 2 == 0:
-                    y[nb, h] = held.tile([P, HALF], F32, name="y%d%d" % (nb, h), align_bytes=DMA_ALIGN)
-                acc = psum.tile([P, C], F32, name="acc%d%d" % (e, nb))
-                for g in range(PASSES):
-                    nc.tensor.matmul_mx(
-                        out=acc[:],
-                        lhsT=w_codes[g][:, nb * P : (nb + 1) * P].bitcast(FP8X4),
-                        lhsT_scale=w_scales[g][:, nb * P : (nb + 1) * P],
-                        rhs=x_codes[g][:, e * C : (e + 1) * C].bitcast(FP8X4),
-                        rhs_scale=x_scales[g][:, e * C : (e + 1) * C],
-                        start=(g == 0),
-                        stop=(g == PASSES - 1),
-                    )
-                nc.scalar.activation(
-                    out=y[nb, h][:, lo : lo + C], in_=acc[:], func=SILU, bias=bias[:, nb, e : e + 1], scale=1.0
-                )
-            for nb, hh in SCATTERS_AFTER[e]:
-                nc.vector.tensor_tensor(
-                    out=window[nb][:].indirect(offs_sb[:, hh * COLS : (hh + 1) * COLS]),
-                    in0=y[nb, hh][:],
-                    in1=gate_sb[nb][:, hh * HALF : (hh + 1) * HALF],
-                    op=MULT,
-                )
-                if hh == HALVES - 1:
-                    nc.sync.dma_start(out=out[nb * P : (nb + 1) * P, :], in_=window[nb][:])
+            lo = (e % 2) * C
+            nc.scalar.activation(
+                out=y[e // 2, nb][:, lo : lo + C], in_=acc[:], func=SILU, bias=bias[:, nb, e : e + 1], scale=1.0
+            )
+
+        done = {nb: 0 for nb in range(BLOCKS)}
+
+        def scatter(h, nb):
+            nc.vector.tensor_tensor(
+                out=window[nb][:].indirect(offs_sb[:, h * COLS : (h + 1) * COLS]),
+                in0=y[h, nb][:],
+                in1=gate_sb[nb][:, h * HALF : (h + 1) * HALF],
+                op=MULT,
+            )
+            done[nb] += 1
+            if done[nb] == HALVES:
+                nc.sync.dma_start(out=out[nb * P : (nb + 1) * P, :], in_=window[nb][:])
+
+        calls = {
+            "gather": gather,
+            "interleave": interleave,
+            "xq": quantise_tokens,
+            "cw": copy_whole,
+            "qw": quantise_whole,
+            "cb": copy_block,
+            "qb": quantise_block,
+            "mm": multiply,
+            "scatter": scatter,
+        }
+        for item in TOKENS + WORK:
+            calls[item[0]](*item[1:])

from contextlib import ExitStack

import concourse.mybir as mybir

K, T, E, C, N = 1024, 2048, 4, 128, 256
FLOPS = 2 * K * N * E * C

F32 = mybir.dt.float32
BF16 = mybir.dt.bfloat16
U32 = mybir.dt.uint32
U16 = mybir.dt.uint16
U8 = mybir.dt.uint8
FP8X4 = mybir.dt.float8_e4m3fn_x4
SILU = mybir.ActivationFunctionType.Silu
MULT = mybir.AluOpType.mult

P = 128
PACK = 4
K_PASS = P * PACK
PASSES = K // K_PASS
BLOCKS = N // P
SLOTS = E * C
RUN = 8
HALF = 256
HALVES = SLOTS // HALF
COLS = HALF // 16
DMA_ALIGN = 256
DIRECT = (False, True)
LOADS = (
    ("x", 0, 0),
    ("x", 0, 1),
    ("x", 0, 2),
    ("x", 0, 3),
    ("x", 1, 0),
    ("x", 1, 1),
    ("x", 1, 2),
    ("x", 1, 3),
    (0, None),
    (1, None),
    ("gate", 0, 0, 2),
    (2, None),
    (3, 0),
    (3, 1),
    ("gate", 1, 0, 2),
)
TOKENS = (
    ("gather", 0, 0, 0, 2),
    ("gather", 0, 1, 0, 2),
    ("gather", 0, 2, 0, 2),
    ("gather", 0, 3, 0, 2),
    ("interleave", 0),
    ("xq", 0, 0, 2),
    ("gather", 1, 0, 0, 2),
    ("gather", 1, 1, 0, 2),
    ("gather", 1, 2, 0, 2),
    ("gather", 1, 3, 0, 2),
    ("xq", 1, 0, 2),
)
WORK = (
    ("cw", 0, 0, "s"),
    ("qw", 0, 0),
    ("cw", 0, 1, "s"),
    ("qw", 0, 1),
    ("mm", 0, 0),
    ("mm", 0, 1),
    ("cw", 1, 0, "s"),
    ("qw", 1, 0),
    ("cw", 1, 1, "v"),
    ("qw", 1, 1),
    ("mm", 1, 0),
    ("mm", 1, 1),
    ("scatter", 0, 0),
    ("cw", 2, 0, "v"),
    ("qw", 2, 0),
    ("cw", 2, 1, "s"),
    ("qw", 2, 1),
    ("mm", 2, 0),
    ("mm", 2, 1),
    ("cb", 3, 0, 0, 2, "s"),
    ("qb", 3, 0, 0, 2),
    ("mm", 3, 0),
    ("scatter", 0, 1),
    ("cb", 3, 1, 0, 2, "s"),
    ("qb", 3, 1, 0, 2),
    ("mm", 3, 1),
    ("scatter", 1, 0),
    ("scatter", 1, 1),
)
TURN = (1, 0)


def tile_routed_moe_kernel(tc, xT, w, b, gate, offs, out):
    nc = tc.nc
    with ExitStack() as ctx:
        held = ctx.enter_context(tc.tile_pool(name="held", bufs=1))
        psum = ctx.enter_context(tc.psum_pool(name="psum", bufs=1))

        offs_sb = held.tile([P, SLOTS // 16], U16, name="offs_sb")
        nc.sync.dma_start(offs_sb[:], offs)

        bias = held.tile([P, BLOCKS, E], F32, name="bias", align_bytes=DMA_ALIGN)
        nc.scalar.dma_start(out=bias[:], in_=b.rearrange("(nb p) e -> p nb e", p=P))

        planes = {}
        x_view = xT.rearrange("(g p t) n -> g p t n", p=P, t=PACK)
        w_raw = {}
        gate_sb = {}
        w_view = w.rearrange("e (g p j) n -> e g p j n", p=P, j=PACK)
        for item in LOADS:
            if item[0] == "x":
                g, t = item[1:]
                planes[g, t] = held.tile([P, T], F32, name="plane%d%d" % (g, t), align_bytes=DMA_ALIGN)
                nc.sync.dma_start(out=planes[g, t][:], in_=x_view[g, :, t, :])
            elif item[0] == "gate":
                nb = item[1]
                lo, hi = item[2:]
                if nb not in gate_sb:
                    gate_sb[nb] = held.tile([P, SLOTS], F32, name="gate%d" % nb, align_bytes=DMA_ALIGN)
                nc.sync.dma_start(
                    out=gate_sb[nb][:, lo * HALF : hi * HALF],
                    in_=gate[nb * P : (nb + 1) * P, lo * HALF : hi * HALF],
                )
            elif item[1] is None:
                e = item[0]
                for g in range(PASSES):
                    w_raw[e, g, None] = held.tile([P, PACK, N], F32, name="wraw%d_%d" % (e, g), align_bytes=DMA_ALIGN)
                    nc.sync.dma_start(out=w_raw[e, g, None][:], in_=w_view[e, g])
            else:
                e, nb = item
                for g in range(PASSES):
                    if (e, nb) not in w_raw:
                        w_raw[e, nb] = held.tile([P, PASSES, PACK, P], F32, name="wraw%d%d" % (e, nb), align_bytes=DMA_ALIGN)
                    nc.sync.dma_start(
                        out=w_raw[e, nb][:, g, :, :], in_=w_view[e, g, :, :, nb * P : (nb + 1) * P]
                    )

        warm = held.tile([P, 1], F32, name="warm")
        warm2 = held.tile([P, 1], F32, name="warm2")
        nc.vector.memset(warm[:], 0.0)
        nc.scalar.activation(out=warm2[:], in_=warm[:], func=SILU)
        window = {}
        for nb in range(BLOCKS):
            window[nb] = held.tile([P, T], F32, name="window%d" % nb, align_bytes=DMA_ALIGN)
            nc.vector.memset(window[nb][:], 0.0)

        engines = {"v": nc.vector, "s": nc.scalar, "a": nc.any, "p": nc.gpsimd}

        def copy(engine, out_view, in_view):
            if engine == "s":
                nc.scalar.copy(out=out_view, in_=in_view)
            elif engine == "p":
                nc.gpsimd.tensor_scalar(
                    out=out_view, in0=in_view, scalar1=1.0, scalar2=0.0, op0=MULT, op1=mybir.AluOpType.add
                )
            else:
                engines[engine].tensor_copy(out=out_view, in_=in_view)

        x_grouped = {}
        x_codes = {}
        x_scales = {}
        picked = held.tile([P, PACK, SLOTS], F32, name="picked0", align_bytes=DMA_ALIGN)
        for g in range(PASSES):
            x_grouped[g] = held.tile([P, SLOTS, PACK], BF16, name="xg%d" % g, align_bytes=DMA_ALIGN)
        y = {}
        for h in range(HALVES):
            for nb in range(BLOCKS):
                y[h, nb] = held.tile([P, HALF], F32, name="y%d%d" % (nb, h), align_bytes=DMA_ALIGN)
        grouped = {}
        codes = {}
        scales = {}

        def gather(g, t, lo, hi):
            s = slice(lo * HALF, hi * HALF)
            nc.vector.tensor_copy(
                out=x_grouped[g][:, s, t] if g == 1 else picked[:, t, s],
                in_=planes[g, t][:].indirect(offs_sb[:, lo * COLS : hi * COLS]),
            )

        def interleave(g):
            nc.scalar.copy(
                out=x_grouped[g][:].rearrange("p (c i) t -> p c t i", i=RUN),
                in_=picked[:].rearrange("p t (c i) -> p c t i", i=RUN),
            )

        def quantise_tokens(g, lo, hi, pinned=False):
            s = slice(lo * HALF, hi * HALF)
            width = (hi - lo) * HALF
            if pinned:
                xc = held.tile([P, width], U32, name="xc%d%d" % (g, lo), tag="turn", align_bytes=DMA_ALIGN)
            else:
                xc = held.tile([P, width], U32, name="xc%d%d" % (g, lo), align_bytes=DMA_ALIGN)
            xs = held.tile([P, width], U8, name="xs%d%d" % (g, lo), align_bytes=DMA_ALIGN)
            nc.vector.quantize_mx(
                out=xc[:].bitcast(FP8X4),
                scales=xs[:],
                in_=x_grouped[g][:, s, :].rearrange("p c t -> p (c t)"),
            )
            for h in range(lo, hi):
                x_codes[g, h] = xc[:, (h - lo) * HALF : (h - lo + 1) * HALF]
                x_scales[g, h] = xs[:, (h - lo) * HALF : (h - lo + 1) * HALF]

        def copy_whole(e, g, engine):
            grouped[e, g, None] = held.tile([P, N, PACK], BF16, name="wg%d_%d" % (e, g), align_bytes=DMA_ALIGN)
            copy(
                engine,
                grouped[e, g, None][:].rearrange("p (c i) j -> p c j i", i=RUN),
                w_raw[e, g, None][:].rearrange("p j (c i) -> p c j i", i=RUN),
            )

        def quantise_whole(e, g):
            codes[e, g, None] = held.tile([P, N], U32, name="wc%d_%d" % (e, g), align_bytes=DMA_ALIGN)
            scales[e, g, None] = held.tile([P, N], U8, name="ws%d_%d" % (e, g), align_bytes=DMA_ALIGN)
            nc.vector.quantize_mx(
                out=codes[e, g, None][:].bitcast(FP8X4),
                scales=scales[e, g, None][:],
                in_=grouped[e, g, None][:].rearrange("p n j -> p (n j)"),
            )

        def copy_block(e, nb, lo, hi, engine):
            if (e, nb) not in grouped:
                if (e, nb) == TURN:
                    grouped[e, nb] = held.tile([P, PASSES, P, PACK], BF16, name="wg%d%d" % (e, nb), tag="turn", align_bytes=DMA_ALIGN)
                else:
                    grouped[e, nb] = held.tile([P, PASSES, P, PACK], BF16, name="wg%d%d" % (e, nb), align_bytes=DMA_ALIGN)
            copy(
                engine,
                grouped[e, nb][:, lo:hi].rearrange("p g (c i) j -> p g c j i", i=RUN),
                w_raw[e, nb][:, lo:hi].rearrange("p g j (c i) -> p g c j i", i=RUN),
            )

        def quantise_block(e, nb, lo, hi):
            if (e, nb) not in codes:
                codes[e, nb] = held.tile([P, PASSES * P], U32, name="wc%d%d" % (e, nb), align_bytes=DMA_ALIGN)
                scales[e, nb] = held.tile([P, PASSES * P], U8, name="ws%d%d" % (e, nb), align_bytes=DMA_ALIGN)
            s = slice(lo * P, hi * P)
            nc.vector.quantize_mx(
                out=codes[e, nb][:, s].bitcast(FP8X4),
                scales=scales[e, nb][:, s],
                in_=grouped[e, nb][:, lo:hi].rearrange("p g n j -> p (g n j)"),
            )

        def multiply(e, nb):
            acc = psum.tile([P, C], F32, name="acc%d%d" % (e, nb))
            for g in range(PASSES):
                if (e, nb) in codes:
                    key, s = (e, nb), slice(g * P, (g + 1) * P)
                else:
                    key, s = (e, g, None), slice(nb * P, (nb + 1) * P)
                nc.tensor.matmul_mx(
                    out=acc[:],
                    lhsT=codes[key][:, s].bitcast(FP8X4),
                    lhsT_scale=scales[key][:, s],
                    rhs=x_codes[g, e // 2][:, (e % 2) * C : (e % 2 + 1) * C].bitcast(FP8X4),
                    rhs_scale=x_scales[g, e // 2][:, (e % 2) * C : (e % 2 + 1) * C],
                    start=(g == 0),
                    stop=(g == PASSES - 1),
                )
            lo = (e % 2) * C
            nc.scalar.activation(
                out=y[e // 2, nb][:, lo : lo + C], in_=acc[:], func=SILU, bias=bias[:, nb, e : e + 1], scale=1.0
            )

        done = {nb: 0 for nb in range(BLOCKS)}

        def scatter(h, nb):
            nc.vector.tensor_tensor(
                out=window[nb][:].indirect(offs_sb[:, h * COLS : (h + 1) * COLS]),
                in0=y[h, nb][:],
                in1=gate_sb[nb][:, h * HALF : (h + 1) * HALF],
                op=MULT,
            )
            done[nb] += 1
            if done[nb] == HALVES:
                nc.sync.dma_start(out=out[nb * P : (nb + 1) * P, :], in_=window[nb][:])

        calls = {
            "gather": gather,
            "interleave": interleave,
            "xq": quantise_tokens,
            "cw": copy_whole,
            "qw": quantise_whole,
            "cb": copy_block,
            "qb": quantise_block,
            "mm": multiply,
            "scatter": scatter,
        }
        for item in TOKENS + WORK:
            calls[item[0]](*item[1:])
